import numpy as np
import ml_dtypes


def mxq(x, axis, fmt="e4m3"):
    dtype, down = {"e4m3": (ml_dtypes.float8_e4m3fn, 7), "e5m2": (ml_dtypes.float8_e5m2, 14)}[fmt]
    v = np.moveaxis(np.asarray(x, np.float32).astype(ml_dtypes.bfloat16).astype(np.float64), axis, -1)
    blocks = v.reshape(v.shape[:-1] + (-1, 32))
    amax = np.abs(blocks).max(-1, keepdims=True)
    byte = np.maximum(np.where(amax > 0, np.frexp(amax)[1] - 1 + 127, 0) - down, 1)
    scale = np.exp2(byte - 127.0)
    codes = (blocks / scale).astype(np.float32).astype(dtype).astype(np.float64)
    return np.moveaxis((codes * scale).reshape(v.shape), -1, axis)


WIDE = False


def mx_kscale(k):
    if not WIDE:
        return np.ones(k)
    levels = np.array([30, -30])
    if k % 512:
        return np.exp2(np.random.permutation(np.resize(levels, k // 32))).repeat(32)
    a = np.empty((k // 512, 16))
    for p in range(k // 512):
        a[p, :8] = np.random.permutation(np.resize(levels, 8))
        for g in range(8):
            far = levels[np.abs(levels - a[p, g]) >= 10]
            a[p, g + 8] = far[np.random.randint(len(far))]
    return np.exp2(a.ravel()).repeat(32)


def f64(x):
    return np.asarray(x).astype(np.float64)


def striped(idx):
    return np.tile(np.asarray(idx).reshape(-1, 16).T, (8, 1)).astype(np.uint16)


def unstriped(offs):
    return offs[:16].T.reshape(-1).astype(np.int64)


def striped8(idx):
    return np.asarray(idx).reshape(8, -1, 16).transpose(0, 2, 1).reshape(128, -1).astype(np.uint16)


def unstriped8(offs):
    return offs.reshape(8, 16, -1).transpose(0, 2, 1).reshape(8, -1).astype(np.int64)


def pick8(x, idx, run):
    r = np.arange(len(x))
    return x[r[:, None], idx[r % (8 * run) // run]]


E2M1 = np.array([0.0, 0.5, 1.0, 1.5, 2.0, 3.0, 4.0, 6.0, -0.0, -0.5, -1.0, -1.5, -2.0, -3.0, -4.0, -6.0])


def pack_weight(w, fmt):
    k, n = w.shape
    w = f64(np.asarray(w, np.float32).astype(ml_dtypes.bfloat16)).reshape(k // 32, 32, n)
    amax = np.abs(w).max(1)
    if fmt in ("e4m3", "e5m2"):
        byte = np.frexp(amax)[1] - 1 + 127 - (7 if fmt == "e4m3" else 14)
    else:
        mant, ex = np.frexp(amax / 6.0)
        byte = np.where(mant > 0.5, ex, ex - 1) + 127
    byte = np.clip(np.where(amax > 0, byte, 1), 1, 254)
    scaled = (w * np.exp2(127.0 - byte)[:, None, :]).reshape(k, n).astype(np.float32)
    by_word = np.ascontiguousarray(scaled.reshape(k // 512, 128, 4, n).transpose(0, 1, 3, 2))
    if fmt in ("e4m3", "e5m2"):
        words = by_word.astype(ml_dtypes.float8_e4m3fn if fmt == "e4m3" else ml_dtypes.float8_e5m2).view(np.uint8)
    else:
        c = by_word.astype(ml_dtypes.float4_e2m1fn).view(np.uint8) & 0xF
        words = (c[..., 0::2] | (c[..., 1::2] << 4)).reshape(k // 512, 128, 2 * n)
    return np.ascontiguousarray(words), np.ascontiguousarray(byte.astype(np.uint8).reshape(k // 512, 16, n))


def unpack_weight(words, scales, fmt):
    g, _, n = scales.shape
    words = np.ascontiguousarray(words).reshape(g, 128, n, -1)
    if fmt in ("e4m3", "e5m2"):
        vals = words.view(ml_dtypes.float8_e4m3fn if fmt == "e4m3" else ml_dtypes.float8_e5m2).astype(np.float64)
    else:
        nib = np.empty((g, 128, n, 4), np.uint8)
        nib[..., 0::2] = words & 0xF
        nib[..., 1::2] = words >> 4
        vals = E2M1[nib]
    vals = vals * np.repeat(np.exp2(scales.astype(np.float64) - 127.0), 8, axis=1)[..., None]
    return vals.transpose(0, 1, 3, 2).reshape(g * 512, n)


def sgn(shape):
    return np.random.uniform(0.5, 2.0, shape) * np.where(np.random.standard_normal(shape) < 0, -1.0, 1.0)


K, T, J, R, F, Z, C, I, O, N, E = 512, 1024, 256, 512, 512, 1024, 512, 256, 128, 256, 512


def setup_inputs():
    n = np.random.standard_normal
    idx = np.random.permutation(T)[:J]
    idx2 = np.random.permutation(Z)[:J]
    idx3 = np.stack([np.random.permutation(C)[:J] for _ in range(8)])
    idx4 = np.stack([np.random.permutation(C)[:I] for _ in range(8)])
    idx5 = np.random.permutation(T)[:O]
    idx6 = np.random.permutation(E)[:O]
    idx7 = np.random.permutation(E)[:O]
    fk = mx_kscale(K)
    ff = mx_kscale(F)
    fr = mx_kscale(R)
    xtp = pack_weight(n((K, T)) / fk[:, None], "e2m1")
    xop = pack_weight(n((F, Z)) / ff[:, None], "e5m2")
    wp = pack_weight(n((K, R)) * 1 / np.sqrt(K) * fk[:, None] * fr, "e5m2")
    w0p = pack_weight(n((F, R)) * 1 / np.sqrt(F) * ff[:, None] * fr, "e4m3")
    wbp = pack_weight(n((R, N)) * 1 / np.sqrt(R) / fr[:, None], "e4m3")
    wsp = pack_weight(n((K, N)) * 1 / np.sqrt(K) * fk[:, None], "e4m3")
    return {
        "xt_words": xtp[0],
        "xt_scales": xtp[1],
        "xo_words": xop[0],
        "xo_scales": xop[1],
        "w_words": wp[0],
        "w_scales": wp[1],
        "w0_words": w0p[0],
        "w0_scales": w0p[1],
        "sa": (sgn((R, 1))).astype(np.float32),
        "wb_words": wbp[0],
        "wb_scales": wbp[1],
        "ws_words": wsp[0],
        "ws_scales": wsp[1],
        "offs": striped(idx),
        "offs2": striped(idx2),
        "offs3": striped8(idx3),
        "offs4": striped8(idx4),
        "offs5": striped(idx5),
        "offs6": striped(idx6),
        "offs7": striped(idx7),
    }


def reference(xt_words, xt_scales, xo_words, xo_scales, w_words, w_scales, w0_words, w0_scales, sa, wb_words, wb_scales, ws_words, ws_scales, offs, offs2, offs3, offs4, offs5, offs6, offs7):
    idx = unstriped(offs)
    idx2 = unstriped(offs2)
    idx3 = unstriped8(offs3)
    idx4 = unstriped8(offs4)
    idx5 = unstriped(offs5)
    idx6 = unstriped(offs6)
    idx7 = unstriped(offs7)
    xtu = unpack_weight(xt_words, xt_scales, "e2m1")
    xou = unpack_weight(xo_words, xo_scales, "e5m2")
    wu = unpack_weight(w_words, w_scales, "e5m2")
    w0u = unpack_weight(w0_words, w0_scales, "e4m3")
    wbu = unpack_weight(wb_words, wb_scales, "e4m3")
    wsu = unpack_weight(ws_words, ws_scales, "e4m3")
    xtidxg = xtu[:, idx]
    xoidx2g = xou[:, idx2]
    a = wu.T @ xtidxg + w0u.T @ xoidx2g
    pw = np.zeros((R, C))
    pw[np.arange(R)[:, None], idx3[np.arange(R) % 512 // 64]] = a
    h1 = pick8(pw, idx4, 64) * f64(sa)
    hid = h1.reshape(R, O, I // O).max(axis=2)
    hidq = mxq(hid, 0, "e5m2")
    xtidx5g = xtu[:, idx5]
    p = wbu.T @ hidq + wsu.T @ xtidx5g
    pa = np.zeros((N, E))
    pa[:, idx6] = p
    pb = np.zeros((N, E))
    pb[:, idx7] = p
    y = pa + pb
    return y

from contextlib import ExitStack

import concourse.mybir as mybir

K, T, J, R, F, Z, C, I, O, N, E = 512, 1024, 256, 512, 512, 1024, 512, 256, 128, 256, 512
FLOPS = 2 * K * R * J + 2 * F * R * J + 2 * R * N * O + 2 * K * N * O

F32 = mybir.dt.float32
BF16 = mybir.dt.bfloat16
I32 = mybir.dt.int32
U32 = mybir.dt.uint32
U16 = mybir.dt.uint16
U8 = mybir.dt.uint8
E4M3 = mybir.dt.float8_e4m3fn_x4
E5M2 = mybir.dt.float8_e5m2_x4
E2M1 = mybir.dt.float4_e2m1fn_x4
COPY = mybir.ActivationFunctionType.Copy
ALU = mybir.AluOpType

P = 128
PACK = 4
HALF = J // 2


def words_i32(words):
    return words[0].rearrange("p n t -> p (n t)").bitcast(I32)


def load_rows(queue, rows, scales):
    queue.dma_start(
        out=rows[:].bitcast(I32).rearrange("r (q n) -> r q n", q=4),
        in_=scales[0].bitcast(I32).rearrange("(q r) n -> r q n", q=4),
    )


def load_plane(queue, plane, scales):
    for quad in range(4):
        queue.dma_start(out=plane[32 * quad : 32 * quad + 4, :].bitcast(I32), in_=scales[0].bitcast(I32)[4 * quad : 4 * quad + 4, :])


def tile_list_ownpool_bank_further_pagetwice_kernel(
    tc, xt_words, xt_scales, xo_words, xo_scales, w_words, w_scales, w0_words, w0_scales, sa,
    wb_words, wb_scales, ws_words, ws_scales, offs, offs2, offs3, offs4, offs5, offs6, offs7, out,
):
    nc = tc.nc
    with ExitStack() as ctx:
        lists = ctx.enter_context(tc.tile_pool(name="lists", bufs=1))
        sb = ctx.enter_context(tc.tile_pool(name="sb", bufs=1))
        psum = ctx.enter_context(tc.psum_pool(name="psum", bufs=1))

        shared = ctx.enter_context(tc.tile_pool(name="shared", bufs=1))

        def tile(name, shape, dtype, tag=None):
            return sb.tile(shape, dtype, name=name, tag=tag or name, align_bytes=64)

        def gathered(name, half, dtype, offset):
            if half == 0:
                return tile(name + "0", [P, HALF], dtype)
            return shared.tile([P, HALF], dtype, name=name + "1", align_bytes=64, offset=offset)

        l1 = lists.tile([P, J // 16], U16, name="l1")
        l2 = lists.tile([P, J // 16], U16, name="l2")
        l3 = lists.tile([P, J // 16], U16, name="l3")
        l4 = lists.tile([P, I // 16], U16, name="l4")
        l5 = lists.tile([P, O // 16], U16, name="l5")
        l6 = lists.tile([P, O // 16], U16, name="l6")
        l7 = lists.tile([P, O // 16], U16, name="l7")

        xtw = tile("xtw", [P, T], U16)
        xow = tile("xow", [P, Z], U32)
        xts_rows = tile("xts_rows", [4, 4 * T], U8)
        ws_rows = tile("wsc_rows", [4, 4 * R], U8)
        w0s_rows = tile("w0sc_rows", [4, 4 * R], U8)
        xts = tile("xts", [P, T], U8)
        xos = tile("xos", [P, Z], U8)
        w_raw = tile("w_raw", [P, R], U32)
        w0_raw = shared.tile([P, R], U32, name="w0_raw", align_bytes=64, offset=0)
        ws_raw = tile("wsc_raw", [P, R], U8)
        w0s_raw = tile("w0sc_raw", [P, R], U8)
        wbw = tile("wbw", [P, N], U32)
        wsw = tile("wsw", [P, N], U32)
        wbs = tile("wbs", [P, N], U8)
        wss = tile("wss", [P, N], U8)
        sa_t = tile("sa_t", [P, PACK], F32)
        board = [tile("board%d" % t, [P, C], F32) for t in range(PACK)]

        for plane in (xos, xts, ws_raw, w0s_raw):
            nc.vector.memset(plane[:].bitcast(I32), 0)
        for t in range(PACK):
            nc.vector.memset(board[t][:], 0.0)
        nc.gpsimd.memset(wss[:].bitcast(I32), 0)
        nc.gpsimd.memset(wbs[:].bitcast(I32), 0)

        nc.sync.dma_start(l1[:], offs)
        load_rows(nc.scalar, xts_rows, xt_scales)
        nc.sync.dma_start(l2[:], offs2)
        load_rows(nc.scalar, ws_rows, w_scales)
        nc.sync.dma_start(out=xtw[:].bitcast(I32), in_=xt_words[0].bitcast(I32))
        load_rows(nc.scalar, w0s_rows, w0_scales)
        nc.sync.dma_start(out=xow[:].bitcast(I32), in_=words_i32(xo_words))
        nc.scalar.dma_start(out=w_raw[:].bitcast(I32), in_=words_i32(w_words))
        load_plane(nc.sync, xos, xo_scales)
        nc.sync.dma_start(out=w0_raw[:].bitcast(I32), in_=words_i32(w0_words))
        nc.sync.dma_start(l3[:], offs3)
        nc.sync.dma_start(l4[:], offs4)
        nc.sync.dma_start(l5[:], offs5)
        nc.sync.dma_start(out=wsw[:].bitcast(I32), in_=words_i32(ws_words))
        load_plane(nc.sync, wss, ws_scales)
        nc.sync.dma_start(out=wbw[:].bitcast(I32), in_=words_i32(wb_words))
        load_plane(nc.sync, wbs, wb_scales)
        nc.sync.dma_start(l6[:], offs6)
        nc.sync.dma_start(l7[:], offs7)
        nc.sync.dma_start(out=sa_t[:], in_=sa.rearrange("(p t) one -> p (t one)", t=PACK))

        for quad in range(4):
            for rows, plane in ((xts_rows, xts), (ws_rows, ws_raw), (w0s_rows, w0s_raw)):
                width = plane.shape[1] // 4
                nc.vector.tensor_copy(
                    out=plane[32 * quad : 32 * quad + 4, :].bitcast(I32),
                    in_=rows[:].bitcast(I32)[:, quad * width : (quad + 1) * width],
                )

        def slices(first, rest):
            return [first[:]] + [rest[:, (t - 1) * P : t * P] for t in range(1, PACK)]

        dealt_scales = []
        for name, raw in (("wps", ws_raw), ("w0ps", w0s_raw)):
            first = tile(name + "0", [P, P], U8)
            rest = tile(name + "r", [P, (PACK - 1) * P], U8)
            by_t = raw[:].rearrange("p (m t) -> p t m", t=PACK)
            nc.vector.tensor_copy(out=first[:], in_=by_t[:, 0, :])
            nc.gpsimd.tensor_copy(out=rest[:].rearrange("p (t m) -> p t m", m=P), in_=by_t[:, 1:, :])
            dealt_scales.append(slices(first, rest))
        wps, w0ps = dealt_scales
        w_all = tile("wp", [P, R], U32)
        nc.scalar.copy(out=w_all[:].rearrange("p (t m) -> p m t", t=PACK), in_=w_raw[:].rearrange("p (m t) -> p m t", t=PACK))
        wp = [w_all[:, t * P : (t + 1) * P] for t in range(PACK)]
        first = tile("w0p0", [P, P], U32)
        rest = tile("w0pr", [P, (PACK - 1) * P], U32)
        by_m = w0_raw[:].rearrange("p (m t) -> p m t", t=PACK)
        nc.scalar.copy(out=first[:], in_=by_m[:, :, 0])
        nc.scalar.copy(out=rest[:].rearrange("p (t m) -> p m t", m=P), in_=by_m[:, :, 1:])
        w0p = slices(first, rest)

        for half in range(2):
            cols = slice(half * HALF // 16, (half + 1) * HALF // 16)
            xtg = gathered("xtg", half, U16, 0)
            xtgs = gathered("xtgs", half, U8, 2 * HALF)
            xog = gathered("xog", half, U32, 4 * HALF)
            xogs = gathered("xogs", half, U8, 3 * HALF)
            nc.vector.tensor_copy(xtg[:], xtw[:].indirect(l1[:, cols]))
            nc.vector.tensor_copy(xtgs[:], xts[:].indirect(l1[:, cols]))
            nc.vector.tensor_copy(xog[:], xow[:].indirect(l2[:, cols]))
            nc.vector.tensor_copy(xogs[:], xos[:].indirect(l2[:, cols]))
            for t in range(PACK):
                acc = psum.tile([P, HALF], F32, name="acc%d%d" % (half, t), tag="bank%d" % (half * PACK + t))
                nc.tensor.matmul_mx(
                    out=acc[:], lhsT=wp[t].bitcast(E5M2), lhsT_scale=wps[t],
                    rhs=xtg[:].bitcast(E2M1), rhs_scale=xtgs[:], start=True, stop=False,
                )
                nc.tensor.matmul_mx(
                    out=acc[:], lhsT=w0p[t].bitcast(E4M3), lhsT_scale=w0ps[t],
                    rhs=xog[:].bitcast(E5M2), rhs_scale=xogs[:], start=False, stop=True,
                )
                a = tile("a%d%d" % (half, t), [P, HALF], F32)
                if half == 0 and t == 0:
                    nc.scalar.copy(out=a[:], in_=acc[:])
                else:
                    nc.vector.tensor_copy(out=a[:], in_=acc[:])
                nc.scalar.activation(board[t][:].indirect(l3[:, cols]), a[:], COPY)

        xt5 = tile("xt5", [P, O], U16)
        xt5s = tile("xt5s", [P, O], U8)
        nc.vector.tensor_copy(xt5[:], xtw[:].indirect(l5[:]))
        nc.vector.tensor_copy(xt5s[:], xts[:].indirect(l5[:]))

        tiles_n = range(N // P)
        short_acc = psum.tile([P, N // P, O], F32, name="short_acc", tag="bank0")
        for u in tiles_n:
            m = slice(u * P, (u + 1) * P)
            nc.tensor.matmul_mx(
                out=short_acc[:, u, :], lhsT=wsw[:, m].bitcast(E4M3), lhsT_scale=wss[:, m],
                rhs=xt5[:].bitcast(E2M1), rhs_scale=xt5s[:], start=True, stop=True,
            )
        short = tile("short", [P, N // P, O], F32)
        nc.vector.tensor_copy(out=short[:], in_=short_acc[:])

        pa = [tile("pa%d" % u, [P, E], F32, tag="a1%d" % (2 * u)) for u in tiles_n]
        pb = [tile("pb%d" % u, [P, E], F32, tag="a1%d" % (2 * u + 1)) for u in tiles_n]
        for u in tiles_n:
            nc.gpsimd.memset(pa[u][:], 0.0)
            nc.gpsimd.memset(pb[u][:], 0.0)

        OH = O // 2
        hq = tile("hq", [P, 3 * OH], U32)
        hqs = tile("hqs", [P, 3 * OH], U8)
        nc.gpsimd.memset(hq[:, OH : 2 * OH].bitcast(I32), 0)
        nc.gpsimd.memset(hqs[:, OH : 2 * OH].bitcast(I32), 0)
        results = []
        for half in range(2):
            hid = tile("hid%d" % half, [P, OH, PACK], BF16)
            picks = slice(half * I // 32, (half + 1) * I // 32)
            for t in range(PACK):
                h1 = tile("h1_%d%d" % (half, t), [P, I // 2], F32)
                nc.scalar.activation(h1[:], board[t][:].indirect(l4[:, picks]), COPY, scale=sa_t[:, t : t + 1])
                pairs = h1[:].rearrange("p (o two) -> p o two", two=2)
                nc.vector.tensor_tensor(out=hid[:, :, t], in0=pairs[:, :, 0], in1=pairs[:, :, 1], op=ALU.max)
            made = slice(2 * half * OH, (2 * half + 1) * OH)
            nc.vector.quantize_mx(out=hq[:, made].bitcast(E5M2), scales=hqs[:, made], in_=hid[:].rearrange("p o t -> p (o t)"))
            read = slice(half * OH, (half + 2) * OH)
            acc = psum.tile([P, N // P, O], F32, name="pacc%d" % half, tag="bank%d" % (1 + half))
            for u in tiles_n:
                m = slice(u * P, (u + 1) * P)
                nc.tensor.matmul_mx(
                    out=acc[:, u, :], lhsT=wbw[:, m].bitcast(E4M3), lhsT_scale=wbs[:, m],
                    rhs=hq[:, read].bitcast(E5M2), rhs_scale=hqs[:, read], start=True, stop=True,
                )
            pools = slice(half * OH, (half + 1) * OH)
            p = tile("p%d" % half, [P, N // P, OH], F32)
            nc.vector.tensor_tensor(out=p[:], in0=acc[:, :, pools], in1=short[:, :, pools], op=ALU.add)
            results.append(p)

        for half, p in enumerate(results):
            places = slice(half * OH // 16, (half + 1) * OH // 16)
            nc.vector.tensor_copy(pa[0][:].indirect(l6[:, places]), p[:, 0, :])
            nc.scalar.activation(pb[0][:].indirect(l7[:, places]), p[:, 0, :], COPY)
            nc.scalar.activation(pb[1][:].indirect(l7[:, places]), p[:, 1, :], COPY)
            nc.scalar.activation(pa[1][:].indirect(l6[:, places]), p[:, 1, :], COPY)

        for u in tiles_n:
            m = slice(u * P, (u + 1) * P)
            for v, e in enumerate((slice(0, E),) if u == 0 else (slice(0, E // 2), slice(E // 2, E))):
                page = tile("page%d%d" % (u, v), [P, e.stop - e.start], F32)
                nc.vector.tensor_tensor(out=page[:], in0=pa[u][:, e], in1=pb[u][:, e], op=ALU.add)
                (nc.scalar if v == 1 else nc.sync).dma_start(out=out[m, e], in_=page[:])
